import numpy as np
import ml_dtypes


def mxq(x, axis, fmt="e4m3"):
    dtype, down = {"e4m3": (ml_dtypes.float8_e4m3fn, 7), "e5m2": (ml_dtypes.float8_e5m2, 14)}[fmt]
    v = np.moveaxis(np.asarray(x, np.float32).astype(ml_dtypes.bfloat16).astype(np.float64), axis, -1)
    blocks = v.reshape(v.shape[:-1] + (-1, 32))
    amax = np.abs(blocks).max(-1, keepdims=True)
    byte = np.maximum(np.where(amax > 0, np.frexp(amax)[1] - 1 + 127, 0) - down, 1)
    scale = np.exp2(byte - 127.0)
    codes = (blocks / scale).astype(np.float32).astype(dtype).astype(np.float64)
    return np.moveaxis((codes * scale).reshape(v.shape), -1, axis)


WIDE = False


def mx_kscale(k):
    if not WIDE:
        return np.ones(k)
    levels = np.array([10, -10, 5, -5, 0])
    if k % 512:
        return np.exp2(np.random.permutation(np.resize(levels, k // 32))).repeat(32)
    a = np.empty((k // 512, 16))
    for p in range(k // 512):
        a[p, :8] = np.random.permutation(np.resize(levels, 8))
        for g in range(8):
            far = levels[np.abs(levels - a[p, g]) >= 10]
            a[p, g + 8] = far[np.random.randint(len(far))]
    return np.exp2(a.ravel()).repeat(32)


def f64(x):
    return np.asarray(x).astype(np.float64)


def striped(idx):
    return np.tile(idx.reshape(-1, 16).T, (8, 1)).astype(np.uint16)


def unstriped(offs):
    return offs[:16].T.reshape(-1).astype(np.int64)


def striped8(idx):
    return np.concatenate([x.reshape(-1, 16).T for x in idx]).astype(np.uint16)


def runs(offs, k):
    lists = np.stack([offs[16 * r : 16 * r + 16].T.reshape(-1) for r in range(8)]).astype(np.int64)
    return lists[np.arange(k) % 512 // 64]


def pack_weight(w):
    k, n = w.shape
    w = f64(np.asarray(w, np.float32).astype(ml_dtypes.bfloat16)).reshape(k // 32, 32, n)
    amax = np.abs(w).max(1)
    byte = np.clip(np.where(amax > 0, np.frexp(amax)[1] - 1 + 127 - 7, 1), 1, 254)
    scaled = (w * np.exp2(127.0 - byte)[:, None, :]).reshape(k, n).astype(np.float32)
    words = np.ascontiguousarray(scaled.reshape(k // 512, 128, 4, n).transpose(0, 1, 3, 2)).astype(ml_dtypes.float8_e4m3fn).view(np.uint8)
    return words, np.ascontiguousarray(byte.astype(np.uint8).reshape(k // 512, 16, n))


def unpack_weight(words, scales):
    g, p, n, _ = words.shape
    vals = np.ascontiguousarray(words).view(ml_dtypes.float8_e4m3fn).astype(np.float64) * np.repeat(np.exp2(scales.astype(np.float64) - 127.0), 8, axis=1)[..., None]
    return vals.transpose(0, 1, 3, 2).reshape(g * 512, n)


E2M1 = np.array([0.0, 0.5, 1.0, 1.5, 2.0, 3.0, 4.0, 6.0, -0.0, -0.5, -1.0, -1.5, -2.0, -3.0, -4.0, -6.0])


def pack_fp4(w):
    k, n = w.shape
    w = f64(np.asarray(w, np.float32).astype(ml_dtypes.bfloat16)).reshape(k // 32, 32, n)
    amax = np.abs(w).max(1)
    mant, ex = np.frexp(amax / 6.0)
    byte = np.clip(np.where(amax > 0, np.where(mant > 0.5, ex, ex - 1) + 127, 1), 1, 254)
    scaled = (w * np.exp2(127.0 - byte)[:, None, :]).reshape(k, n).astype(np.float32)
    c = np.ascontiguousarray(scaled.reshape(k // 512, 128, 4, n).transpose(0, 1, 3, 2)).astype(ml_dtypes.float4_e2m1fn).view(np.uint8) & 0xF
    words = (c[..., 0::2] | (c[..., 1::2] << 4)).reshape(k // 512, 128, 2 * n)
    return np.ascontiguousarray(words), np.ascontiguousarray(byte.astype(np.uint8).reshape(k // 512, 16, n))


def unpack_fp4(words, scales):
    g, _, n = scales.shape
    words = np.ascontiguousarray(words).reshape(g, 128, n, 2)
    nib = np.empty((g, 128, n, 4), np.uint8)
    nib[..., 0::2] = words & 0xF
    nib[..., 1::2] = words >> 4
    vals = E2M1[nib] * np.repeat(np.exp2(scales.astype(np.float64) - 127.0), 8, axis=1)[..., None]
    return vals.transpose(0, 1, 3, 2).reshape(g * 512, n)


def sigmoid(v):
    return 1.0 / (1.0 + np.exp(-np.maximum(v, -700.0)))


K, T, S, H, W, G = 512, 2048, 512, 512, 256, 2048


def setup_inputs():
    n = np.random.standard_normal
    s = mx_kscale(K)[:, None]
    packed_xT = pack_weight(n((K, T)) * s)
    packed_w1 = pack_fp4(n((K, H)) / np.sqrt(K) / s)
    packed_dT = pack_weight(n((K, G)) / s)
    perm = np.stack([np.random.permutation(S) for _ in range(8)])
    return {
        "x_words": packed_xT[0],
        "x_scales": packed_xT[1],
        "w1_words": packed_w1[0],
        "w1_scales": packed_w1[1],
        "gs": (np.random.uniform(0.5, 1.5, (K, 1)) * s).astype(np.float32),
        "d_words": packed_dT[0],
        "d_scales": packed_dT[1],
        "sl": np.random.uniform(1.0, 2.0, (H, 1)).astype(np.float32),
        "th": (0.5 * n((H, 1))).astype(np.float32),
        "offs": striped(np.random.permutation(T)[:S]),
        "n1": striped8(perm[:, :W]),
        "n2": striped8(perm[:, W:]),
        "ka": striped8(np.random.randint(0, G, (8, H))),
        "kb": striped8(np.random.randint(0, G, (8, H))),
        "n3": striped8(np.stack([np.random.permutation(S) for _ in range(8)])),
    }


def reference(x_words, x_scales, w1_words, w1_scales, gs, d_words, d_scales, sl, th, offs, n1, n2, ka, kb, n3):
    d_ka = unpack_weight(d_words, d_scales)[np.arange(K)[:, None], runs(ka, K)]
    xq = unpack_weight(x_words, x_scales)[:, unstriped(offs)]
    y = unpack_fp4(w1_words, w1_scales).T @ xq
    pb = y[np.arange(H)[:, None], runs(n2, H)]
    pa = y[np.arange(H)[:, None], runs(n1, H)]
    rb = pb - (0.5 * pa)
    ra = np.sqrt((pa) ** 2 + (pb) ** 2 + 0.25)
    ds = np.zeros((H, S))
    ds[np.arange(H)[:, None], runs(n1, H)] = ra
    dt = ds.copy()
    dt[np.arange(H)[:, None], runs(n2, H)] = rb
    z = f64(gs) * dt
    zq = mxq(z, 0, "e4m3")
    d_kb = unpack_weight(d_words, d_scales)[np.arange(K)[:, None], runs(kb, K)]
    h = 0.0625 * (d_ka.T @ zq + d_kb.T @ zq)
    sg = sigmoid(f64(sl) * (h[np.arange(H)[:, None], runs(n3, H)] - f64(th)))
    return h * sg

@@ -1,0 +1,246 @@
+from contextlib import ExitStack
+
+import concourse.mybir as mybir
+
+K, T, S, H, W, G = 512, 2048, 512, 512, 256, 2048
+FLOPS = 3 * 2 * K * H * S
+
+F32 = mybir.dt.float32
+BF16 = mybir.dt.bfloat16
+I32 = mybir.dt.int32
+U32 = mybir.dt.uint32
+U16 = mybir.dt.uint16
+U8 = mybir.dt.uint8
+FP8X4 = mybir.dt.float8_e4m3fn_x4
+FP4X4 = mybir.dt.float4_e2m1fn_x4
+ACT = mybir.ActivationFunctionType
+ALU = mybir.AluOpType
+
+P = 128
+PACK = 4
+QUADS = 4
+HALF = S // 2
+PLANE_ORDER = (2, 0, 1, 3)
+
+
+def tile_picked_daqpolaresa_none_p_kernel(
+    tc, x_words, x_scales, w1_words, w1_scales, gs, d_words, d_scales, sl, th, offs, n1, n2, ka, kb, n3, out
+):
+    nc = tc.nc
+    with ExitStack() as ctx:
+        lists = ctx.enter_context(tc.tile_pool(name="lists", bufs=1))
+        keep = ctx.enter_context(tc.tile_pool(name="keep", bufs=1))
+        psum = ctx.enter_context(tc.psum_pool(name="psum", bufs=1))
+
+        def load_list(name, src):
+            tile = lists.tile(list(src.shape), U16, name=name)
+            nc.sync.dma_start(tile[:], src)
+            return tile
+
+        xs_win = keep.tile([P, T], U8, align_bytes=64)
+        ds_win = keep.tile([P, G], U8, align_bytes=64)
+        w1s_raw = keep.tile([P, H], U8, align_bytes=64)
+        ds_mm = keep.tile([P, 2 * H], U8, align_bytes=64)
+        nc.gpsimd.memset(xs_win[:].bitcast(I32), 0)
+        nc.vector.memset(ds_win[:].bitcast(I32), 0)
+        nc.vector.memset(w1s_raw[:].bitcast(I32), 0)
+        nc.gpsimd.memset(ds_mm[:].bitcast(I32), 0)
+        quarter = keep.tile([P, 1], F32)
+        nc.gpsimd.memset(quarter[:], 0.25)
+
+        xw_win = keep.tile([P, T], U32, align_bytes=64)
+        dw_win = keep.tile([P, G], U32, align_bytes=64)
+        w1w_raw = keep.tile([P, 2 * H], U8, align_bytes=64)
+
+        offs_t = load_list("offs_t", offs)
+        for q in range(QUADS):
+            nc.sync.dma_start(xs_win[32 * q : 32 * q + 4, :].bitcast(I32), x_scales[0, 4 * q : 4 * q + 4, :].bitcast(I32))
+        nc.sync.dma_start(ds_win[0:P:8, :].bitcast(I32), d_scales[0].bitcast(I32))
+        ka_t = load_list("ka_t", ka)
+        nc.sync.dma_start(xw_win[:].bitcast(I32), x_words[0].rearrange("p n t -> p (n t)").bitcast(I32))
+        nc.sync.dma_start(w1w_raw[:].bitcast(I32), w1_words[0].bitcast(I32))
+        for q in range(QUADS):
+            nc.sync.dma_start(w1s_raw[32 * q : 32 * q + 4, :].bitcast(I32), w1_scales[0, 4 * q : 4 * q + 4, :].bitcast(I32))
+        kb_t = load_list("kb_t", kb)
+        nc.sync.dma_start(dw_win[:].bitcast(I32), d_words[0].rearrange("p n t -> p (n t)").bitcast(I32))
+        n1_t = load_list("n1_t", n1)
+        n2_t = load_list("n2_t", n2)
+        n3_t = load_list("n3_t", n3)
+
+        gs_t = keep.tile([P, PACK], F32)
+        sl_t = keep.tile([P, PACK], F32)
+        th_t = keep.tile([P, PACK], F32)
+        for tile, src in ((gs_t, gs), (sl_t, sl), (th_t, th)):
+            nc.sync.dma_start(tile[:], src.rearrange("(p t) o -> p (t o)", t=PACK))
+
+        w1w = keep.tile([P, 2 * H], U8, align_bytes=64)
+        w1s = keep.tile([P, H], U8, align_bytes=64)
+        nc.scalar.copy(
+            w1w[:].bitcast(U16).rearrange("p (t m) -> p t m", t=PACK),
+            w1w_raw[:].bitcast(U16).rearrange("p (m t) -> p t m", t=PACK),
+        )
+        nc.gpsimd.tensor_copy(
+            w1s[:].rearrange("p (t m) -> p t m", t=PACK),
+            w1s_raw[:].rearrange("p (m t) -> p t m", t=PACK),
+        )
+
+        slope_th = keep.tile([P, PACK], F32)
+        neg_bias = keep.tile([P, PACK], F32)
+        nc.gpsimd.tensor_tensor(slope_th[:], sl_t[:], th_t[:], ALU.mult)
+        nc.gpsimd.tensor_scalar(neg_bias[:], slope_th[:], -1.0, 0.0, ALU.mult, ALU.add)
+
+        xs = keep.tile([P, S], U8, align_bytes=64)
+        xw = keep.tile([P, S], U32, align_bytes=64)
+        ds_got = keep.tile([P, 2 * H], U8, align_bytes=64)
+        dw_got = keep.tile([P, 2 * H], U32, align_bytes=64)
+        nc.vector.tensor_copy(xs[:], xs_win[:].indirect(offs_t[:]))
+        nc.vector.tensor_copy(ds_got[:, 0:H], ds_win[:].indirect(ka_t[:]))
+        nc.vector.tensor_copy(xw[:], xw_win[:].indirect(offs_t[:]))
+        nc.vector.tensor_copy(ds_got[:, H : 2 * H], ds_win[:].indirect(kb_t[:]))
+
+        y_ps = {}
+        for t in PLANE_ORDER:
+            y_ps[t] = psum.tile([P, S], F32, name=f"y_ps{t}", tag=f"bank{t}")
+            nc.tensor.matmul_mx(
+                out=y_ps[t][:],
+                lhsT=w1w[:, 2 * P * t : 2 * P * (t + 1)].bitcast(FP4X4),
+                lhsT_scale=w1s[:, P * t : P * (t + 1)],
+                rhs=xw[:].bitcast(FP8X4),
+                rhs_scale=xs[:],
+                start=True,
+                stop=True,
+            )
+
+        ds_dealt = keep.tile([P, 2 * H], U8, align_bytes=64)
+        dw = keep.tile([P, 2 * H], U32, align_bytes=64)
+        nc.vector.tensor_copy(dw_got[:, 0:H], dw_win[:].indirect(ka_t[:]))
+        nc.vector.tensor_copy(
+            ds_dealt[:].rearrange("p (a t m) -> p a t m", a=2, t=PACK),
+            ds_got[:].rearrange("p (a m t) -> p a t m", a=2, t=PACK),
+        )
+        nc.vector.tensor_copy(dw_got[:, H : 2 * H], dw_win[:].indirect(kb_t[:]))
+        for i in range(4):
+            nc.sync.dma_start(ds_mm[i:P:32, :].bitcast(I32), ds_dealt[8 * i : P : 32, :].bitcast(I32))
+
+        zb = keep.tile([P, S, PACK], BF16, align_bytes=64)
+        pair, squares, sums, ra, dt = {}, {}, {}, {}, {}
+
+        def fetch(t):
+            y = keep.tile([P, S], F32, name=f"y{t}")
+            nc.scalar.copy(y[:], y_ps[t][:])
+            pair[t] = keep.tile([P, 2 * W], F32, name=f"pair{t}")
+            nc.scalar.activation(pair[t][:, 0:W], y[:].indirect(n1_t[:]), ACT.Copy, scale=-0.5)
+            nc.scalar.activation(pair[t][:, W : 2 * W], y[:].indirect(n2_t[:]), ACT.Copy)
+            squares[t] = keep.tile([P, 2 * W], F32, name=f"squares{t}")
+            nc.scalar.activation(squares[t][:], pair[t][:], ACT.Square)
+
+        def add_squares(t):
+            sums[t] = keep.tile([P, W], F32, name=f"sums{t}")
+            nc.vector.scalar_tensor_tensor(sums[t][:], squares[t][:, 0:W], 4.0, squares[t][:, W : 2 * W], ALU.mult, ALU.add)
+
+        def root(t):
+            ra[t] = keep.tile([P, W], F32, name=f"ra{t}")
+            nc.scalar.activation(ra[t][:], sums[t][:], ACT.Sqrt, bias=quarter[:])
+
+        def put_rb(t):
+            dt[t] = keep.tile([P, S], F32, name=f"dt{t}", tag=f"dt{min(t, 2)}")
+            nc.vector.tensor_tensor(dt[t][:].indirect(n2_t[:]), pair[t][:, W : 2 * W], pair[t][:, 0:W], ALU.add)
+
+        def put_ra(t):
+            nc.vector.tensor_copy(dt[t][:].indirect(n1_t[:]), ra[t][:])
+
+        def weigh(t):
+            nc.scalar.activation(zb[:, :, t], dt[t][:], ACT.Copy, scale=gs_t[:, t : t + 1])
+
+        a, b, c, d = PLANE_ORDER
+        fetch(a)
+        add_squares(a)
+        nc.vector.tensor_copy(
+            dw[:].rearrange("p (a t m) -> p a m t", a=2, t=PACK),
+            dw_got[:].rearrange("p (a m t) -> p a m t", a=2, t=PACK),
+        )
+        put_rb(a)
+        fetch(b)
+        root(a)
+        add_squares(b)
+        put_rb(b)
+        put_ra(a)
+        fetch(c)
+        root(b)
+        add_squares(c)
+        put_rb(c)
+        put_ra(b)
+        fetch(d)
+        root(c)
+        add_squares(d)
+        weigh(a)
+        root(d)
+        put_rb(d)
+        weigh(b)
+        put_ra(c)
+        weigh(c)
+        put_ra(d)
+
+        zw = keep.tile([P, S], U32, align_bytes=64)
+        zs = keep.tile([P, S], U8, align_bytes=64)
+        halves = [slice(0, HALF), slice(HALF, S)]
+        for cols in halves:
+            nc.vector.tensor_scalar(zb[:, cols, d], dt[d][:, cols], gs_t[:, d : d + 1], None, ALU.mult)
+        for cols in halves:
+            nc.vector.quantize_mx(
+                out=zw[:, cols].bitcast(FP8X4),
+                scales=zs[:, cols],
+                in_=zb[:, cols, :].rearrange("p j t -> p (j t)"),
+            )
+
+        out_rows = out.rearrange("(p t) j -> p t j", t=PACK)
+        h_ps, h, sg, res = {}, {}, {}, {}
+
+        def product(t, cols, bank):
+            for table in range(2):
+                dcols = slice(H * table + P * t, H * table + P * (t + 1))
+                nc.tensor.matmul_mx(
+                    out=bank,
+                    lhsT=dw[:, dcols].bitcast(FP8X4),
+                    lhsT_scale=ds_mm[:, dcols],
+                    rhs=zw[:, cols].bitcast(FP8X4),
+                    rhs_scale=zs[:, cols],
+                    start=(table == 0),
+                    stop=(table == 1),
+                )
+
+        for t in range(PACK):
+            h_ps[t] = []
+            for i, cols in enumerate(halves if t == 0 else [slice(0, S)]):
+                bank = psum.tile([P, cols.stop - cols.start], F32, name=f"h_ps{t}_{i}", tag=f"bank{(4 + t + 4 * i) % 8}")
+                product(t, cols, bank[:])
+                h_ps[t].append((cols, bank))
+
+        def evacuate(t):
+            h[t] = keep.tile([P, S], F32, name=f"h{t}")
+            for cols, bank in h_ps[t]:
+                nc.vector.tensor_scalar(h[t][:, cols], bank[:], 0.0625, None, ALU.mult)
+
+        def gate(t):
+            sg[t] = keep.tile([P, S], F32, name=f"sg{t}")
+            for cols in halves:
+                nc.scalar.activation(
+                    sg[t][:, cols],
+                    h[t][:].indirect(n3_t[:, cols.start // 16 : cols.stop // 16]),
+                    ACT.Sigmoid,
+                    scale=sl_t[:, t : t + 1],
+                    bias=neg_bias[:, t : t + 1],
+                )
+
+        def finish(t):
+            res[t] = keep.tile([P, S], F32, name=f"res{t}")
+            for cols in halves if t == PACK - 1 else [slice(0, S)]:
+                nc.vector.tensor_tensor(res[t][:, cols], h[t][:, cols], sg[t][:, cols], ALU.mult)
+                nc.sync.dma_start(out_rows[:, t, cols], res[t][:, cols])
+
+        evacuate(0)
+        for t in range(PACK):
+            gate(t)
+            if t + 1 < PACK:
+                evacuate(t + 1)
+            finish(t)

@@ -48,6 +48,9 @@ def tile_picked_daqpolaresa_none_p_kernel(
         quarter = keep.tile([P, 1], F32)
         nc.gpsimd.memset(quarter[:], 0.25)
 
+        warm_sqrt = keep.tile([P, 1], F32)
+        nc.scalar.activation(warm_sqrt[:], quarter[:], ACT.Sqrt, bias=quarter[:])
+
         xw_win = keep.tile([P, T], U32, align_bytes=64)
         dw_win = keep.tile([P, G], U32, align_bytes=64)
         w1w_raw = keep.tile([P, 2 * H], U8, align_bytes=64)
@@ -175,6 +178,8 @@ def tile_picked_daqpolaresa_none_p_kernel(
         add_squares(d)
         weigh(a)
         root(d)
+        warm_sigmoid = keep.tile([P, 1], F32)
+        nc.scalar.activation(warm_sigmoid[:], ra[d][:, 0:1], ACT.Sigmoid, bias=quarter[:])
         put_rb(d)
         weigh(b)
         put_ra(c)

@@ -20,7 +20,7 @@ P = 128
 PACK = 4
 QUADS = 4
 HALF = S // 2
-PLANE_ORDER = (2, 0, 1, 3)
+PLANE_ORDER = (0, 1, 2, 3)
 
 
 def tile_picked_daqpolaresa_none_p_kernel(
@@ -52,7 +52,7 @@ def tile_picked_daqpolaresa_none_p_kernel(
         nc.scalar.activation(warm_sqrt[:], quarter[:], ACT.Sqrt, bias=quarter[:])
 
         xw_win = keep.tile([P, T], U32, align_bytes=64)
-        dw_win = keep.tile([P, G], U32, align_bytes=64)
+        dw_win = keep.tile([P, G], U32, align_bytes=64, tag="dw_win")
         w1w_raw = keep.tile([P, 2 * H], U8, align_bytes=64)
 
         offs_t = load_list("offs_t", offs)
@@ -115,7 +115,6 @@ def tile_picked_daqpolaresa_none_p_kernel(
             )
 
         ds_dealt = keep.tile([P, 2 * H], U8, align_bytes=64)
-        dw = keep.tile([P, 2 * H], U32, align_bytes=64)
         nc.vector.tensor_copy(dw_got[:, 0:H], dw_win[:].indirect(ka_t[:]))
         nc.vector.tensor_copy(
             ds_dealt[:].rearrange("p (a t m) -> p a t m", a=2, t=PACK),
@@ -125,72 +124,93 @@ def tile_picked_daqpolaresa_none_p_kernel(
         for i in range(4):
             nc.sync.dma_start(ds_mm[i:P:32, :].bitcast(I32), ds_dealt[8 * i : P : 32, :].bitcast(I32))
 
-        zb = keep.tile([P, S, PACK], BF16, align_bytes=64)
-        pair, squares, sums, ra, dt = {}, {}, {}, {}, {}
+        dw = keep.tile([P, 2 * H], U32, align_bytes=64)
+        nc.vector.tensor_copy(
+            dw[:].rearrange("p (a t m) -> p a m t", a=2, t=PACK),
+            dw_got[:].rearrange("p (a m t) -> p a m t", a=2, t=PACK),
+        )
 
-        def fetch(t):
-            y = keep.tile([P, S], F32, name=f"y{t}")
-            nc.scalar.copy(y[:], y_ps[t][:])
+        wide = {}
+        y, pair, sums, ra, dt = {}, {}, {}, {}, {}
+        a, b, c, d = PLANE_ORDER
+
+        def leave_bank(t):
+            y[t] = keep.tile([P, S], F32, name=f"y{t}", tag=f"y{PLANE_ORDER.index(t) % 2}", align_bytes=64)
+            nc.scalar.copy(y[t][:], y_ps[t][:])
+
+        def fetch_a(t):
             pair[t] = keep.tile([P, 2 * W], F32, name=f"pair{t}")
-            nc.scalar.activation(pair[t][:, 0:W], y[:].indirect(n1_t[:]), ACT.Copy, scale=-0.5)
-            nc.scalar.activation(pair[t][:, W : 2 * W], y[:].indirect(n2_t[:]), ACT.Copy)
-            squares[t] = keep.tile([P, 2 * W], F32, name=f"squares{t}")
-            nc.scalar.activation(squares[t][:], pair[t][:], ACT.Square)
+            nc.scalar.activation(pair[t][:, 0:W], y[t][:].indirect(n1_t[:]), ACT.Copy, scale=-0.5)
 
-        def add_squares(t):
-            sums[t] = keep.tile([P, W], F32, name=f"sums{t}")
-            nc.vector.scalar_tensor_tensor(sums[t][:], squares[t][:, 0:W], 4.0, squares[t][:, W : 2 * W], ALU.mult, ALU.add)
+        def fetch_b(t):
+            nc.scalar.activation(pair[t][:, W : 2 * W], y[t][:].indirect(n2_t[:]), ACT.Copy)
+
+        def square(t):
+            wide[t] = keep.tile([P, 2 * S], F32, name=f"wide{t}")
+            nc.scalar.activation(wide[t][:, S : 2 * S], pair[t][:], ACT.Square)
+            sums[t] = keep.tile([P, W], F32, name=f"sums{t}", tag=f"sums{t}", align_bytes=64)
+            nc.vector.scalar_tensor_tensor(
+                sums[t][:], wide[t][:, S : S + W], 4.0, wide[t][:, S + W : 2 * S], ALU.mult, ALU.add
+            )
 
         def root(t):
             ra[t] = keep.tile([P, W], F32, name=f"ra{t}")
             nc.scalar.activation(ra[t][:], sums[t][:], ACT.Sqrt, bias=quarter[:])
 
         def put_rb(t):
-            dt[t] = keep.tile([P, S], F32, name=f"dt{t}", tag=f"dt{min(t, 2)}")
+            dt[t] = keep.tile([P, S], F32, name=f"dt{t}", tag="dw_win" if t == a else f"dt{t}", align_bytes=64)
             nc.vector.tensor_tensor(dt[t][:].indirect(n2_t[:]), pair[t][:, W : 2 * W], pair[t][:, 0:W], ALU.add)
 
         def put_ra(t):
             nc.vector.tensor_copy(dt[t][:].indirect(n1_t[:]), ra[t][:])
 
-        def weigh(t):
-            nc.scalar.activation(zb[:, :, t], dt[t][:], ACT.Copy, scale=gs_t[:, t : t + 1])
+        def weigh(t, cols):
+            nc.scalar.activation(zb[:, cols, t], dt[t][:, cols], ACT.Copy, scale=gs_t[:, t : t + 1])
 
-        a, b, c, d = PLANE_ORDER
-        fetch(a)
-        add_squares(a)
-        nc.vector.tensor_copy(
-            dw[:].rearrange("p (a t m) -> p a m t", a=2, t=PACK),
-            dw_got[:].rearrange("p (a m t) -> p a m t", a=2, t=PACK),
-        )
+        def weigh_on_vector(t, cols):
+            nc.vector.tensor_scalar(zb[:, cols, t], dt[t][:, cols], gs_t[:, t : t + 1], None, ALU.mult)
+
+        leave_bank(a)
+        leave_bank(b)
+        fetch_a(a)
+        fetch_b(a)
         put_rb(a)
-        fetch(b)
-        root(a)
-        add_squares(b)
+        fetch_a(b)
+        square(a)
+        fetch_b(b)
         put_rb(b)
-        put_ra(a)
-        fetch(c)
-        root(b)
-        add_squares(c)
+        leave_bank(c)
+        square(b)
+        fetch_a(c)
+        fetch_b(c)
         put_rb(c)
-        put_ra(b)
-        fetch(d)
-        root(c)
-        add_squares(d)
-        weigh(a)
-        root(d)
-        warm_sigmoid = keep.tile([P, 1], F32)
-        nc.scalar.activation(warm_sigmoid[:], ra[d][:, 0:1], ACT.Sigmoid, bias=quarter[:])
+        leave_bank(d)
+        square(c)
+        root(a)
+        put_ra(a)
+        fetch_a(d)
+        fetch_b(d)
         put_rb(d)
-        weigh(b)
+        root(b)
+        put_ra(b)
+        square(d)
+        root(c)
         put_ra(c)
-        weigh(c)
+        root(d)
+        halves = [slice(0, HALF), slice(HALF, S)]
+        zb = keep.tile([P, S, PACK], BF16, tag=f"sums{c}", align_bytes=64)
+        weigh(a, slice(0, S))
+        weigh(b, slice(0, S))
+        weigh(c, halves[1])
+        weigh_on_vector(c, halves[0])
         put_ra(d)
+        weigh(d, halves[1])
+        weigh_on_vector(d, halves[0])
+        warm_sigmoid = keep.tile([P, 1], F32)
+        nc.scalar.activation(warm_sigmoid[:], dt[d][:, 0:1], ACT.Sigmoid, bias=quarter[:])
 
         zw = keep.tile([P, S], U32, align_bytes=64)
         zs = keep.tile([P, S], U8, align_bytes=64)
-        halves = [slice(0, HALF), slice(HALF, S)]
-        for cols in halves:
-            nc.vector.tensor_scalar(zb[:, cols, d], dt[d][:, cols], gs_t[:, d : d + 1], None, ALU.mult)
         for cols in halves:
             nc.vector.quantize_mx(
                 out=zw[:, cols].bitcast(FP8X4),
@@ -203,11 +223,11 @@ def tile_picked_daqpolaresa_none_p_kernel(
 
         def product(t, cols, bank):
             for table in range(2):
-                dcols = slice(H * table + P * t, H * table + P * (t + 1))
+                scols = slice(H * table + P * t, H * table + P * (t + 1))
                 nc.tensor.matmul_mx(
                     out=bank,
-                    lhsT=dw[:, dcols].bitcast(FP8X4),
-                    lhsT_scale=ds_mm[:, dcols],
+                    lhsT=dw[:, scols].bitcast(FP8X4),
+                    lhsT_scale=ds_mm[:, scols],
                     rhs=zw[:, cols].bitcast(FP8X4),
                     rhs_scale=zs[:, cols],
                     start=(table == 0),
@@ -222,13 +242,18 @@ def tile_picked_daqpolaresa_none_p_kernel(
                 h_ps[t].append((cols, bank))
 
         def evacuate(t):
-            h[t] = keep.tile([P, S], F32, name=f"h{t}")
+            h[t] = wide[t] if t < PACK - 1 else keep.tile([P, S], F32, name=f"h{t}")
             for cols, bank in h_ps[t]:
                 nc.vector.tensor_scalar(h[t][:, cols], bank[:], 0.0625, None, ALU.mult)
 
+        def pieces(t):
+            if t < PACK - 1:
+                return [slice(0, S)]
+            return [slice(0, HALF), slice(HALF, HALF + P), slice(HALF + P, S)]
+
         def gate(t):
             sg[t] = keep.tile([P, S], F32, name=f"sg{t}")
-            for cols in halves:
+            for cols in pieces(t):
                 nc.scalar.activation(
                     sg[t][:, cols],
                     h[t][:].indirect(n3_t[:, cols.start // 16 : cols.stop // 16]),
@@ -239,7 +264,7 @@ def tile_picked_daqpolaresa_none_p_kernel(
 
         def finish(t):
             res[t] = keep.tile([P, S], F32, name=f"res{t}")
-            for cols in halves if t == PACK - 1 else [slice(0, S)]:
+            for cols in pieces(t):
                 nc.vector.tensor_tensor(res[t][:, cols], h[t][:, cols], sg[t][:, cols], ALU.mult)
                 nc.sync.dma_start(out_rows[:, t, cols], res[t][:, cols])
 

from contextlib import ExitStack

import concourse.mybir as mybir

K, T, S, H, W, G = 512, 2048, 512, 512, 256, 2048
FLOPS = 3 * 2 * K * H * S

F32 = mybir.dt.float32
BF16 = mybir.dt.bfloat16
I32 = mybir.dt.int32
U32 = mybir.dt.uint32
U16 = mybir.dt.uint16
U8 = mybir.dt.uint8
FP8X4 = mybir.dt.float8_e4m3fn_x4
FP4X4 = mybir.dt.float4_e2m1fn_x4
ACT = mybir.ActivationFunctionType
ALU = mybir.AluOpType

P = 128
PACK = 4
QUADS = 4
HALF = S // 2
PLANE_ORDER = (0, 1, 2, 3)


def tile_picked_daqpolaresa_none_p_kernel(
    tc, x_words, x_scales, w1_words, w1_scales, gs, d_words, d_scales, sl, th, offs, n1, n2, ka, kb, n3, out
):
    nc = tc.nc
    with ExitStack() as ctx:
        lists = ctx.enter_context(tc.tile_pool(name="lists", bufs=1))
        keep = ctx.enter_context(tc.tile_pool(name="keep", bufs=1))
        psum = ctx.enter_context(tc.psum_pool(name="psum", bufs=1))

        def load_list(name, src):
            tile = lists.tile(list(src.shape), U16, name=name)
            nc.sync.dma_start(tile[:], src)
            return tile

        xs_win = keep.tile([P, T], U8, align_bytes=64)
        ds_win = keep.tile([P, G], U8, align_bytes=64)
        w1s_raw = keep.tile([P, H], U8, align_bytes=64)
        ds_mm = keep.tile([P, 2 * H], U8, align_bytes=64)
        nc.gpsimd.memset(xs_win[:].bitcast(I32), 0)
        nc.vector.memset(ds_win[:].bitcast(I32), 0)
        nc.vector.memset(w1s_raw[:].bitcast(I32), 0)
        nc.gpsimd.memset(ds_mm[:].bitcast(I32), 0)
        quarter = keep.tile([P, 1], F32)
        nc.gpsimd.memset(quarter[:], 0.25)

        warm_sqrt = keep.tile([P, 1], F32)
        nc.scalar.activation(warm_sqrt[:], quarter[:], ACT.Sqrt, bias=quarter[:])

        xw_win = keep.tile([P, T], U32, align_bytes=64)
        dw_win = keep.tile([P, G], U32, align_bytes=64, tag="dw_win")
        w1w_raw = keep.tile([P, 2 * H], U8, align_bytes=64)

        offs_t = load_list("offs_t", offs)
        for q in range(QUADS):
            nc.sync.dma_start(xs_win[32 * q : 32 * q + 4, :].bitcast(I32), x_scales[0, 4 * q : 4 * q + 4, :].bitcast(I32))
        nc.sync.dma_start(ds_win[0:P:8, :].bitcast(I32), d_scales[0].bitcast(I32))
        ka_t = load_list("ka_t", ka)
        nc.sync.dma_start(xw_win[:].bitcast(I32), x_words[0].rearrange("p n t -> p (n t)").bitcast(I32))
        nc.sync.dma_start(w1w_raw[:].bitcast(I32), w1_words[0].bitcast(I32))
        for q in range(QUADS):
            nc.sync.dma_start(w1s_raw[32 * q : 32 * q + 4, :].bitcast(I32), w1_scales[0, 4 * q : 4 * q + 4, :].bitcast(I32))
        kb_t = load_list("kb_t", kb)
        nc.sync.dma_start(dw_win[:].bitcast(I32), d_words[0].rearrange("p n t -> p (n t)").bitcast(I32))
        n1_t = load_list("n1_t", n1)
        n2_t = load_list("n2_t", n2)
        n3_t = load_list("n3_t", n3)

        gs_t = keep.tile([P, PACK], F32)
        sl_t = keep.tile([P, PACK], F32)
        th_t = keep.tile([P, PACK], F32)
        for tile, src in ((gs_t, gs), (sl_t, sl), (th_t, th)):
            nc.sync.dma_start(tile[:], src.rearrange("(p t) o -> p (t o)", t=PACK))

        w1w = keep.tile([P, 2 * H], U8, align_bytes=64)
        w1s = keep.tile([P, H], U8, align_bytes=64)
        nc.scalar.copy(
            w1w[:].bitcast(U16).rearrange("p (t m) -> p t m", t=PACK),
            w1w_raw[:].bitcast(U16).rearrange("p (m t) -> p t m", t=PACK),
        )
        nc.gpsimd.tensor_copy(
            w1s[:].rearrange("p (t m) -> p t m", t=PACK),
            w1s_raw[:].rearrange("p (m t) -> p t m", t=PACK),
        )

        slope_th = keep.tile([P, PACK], F32)
        neg_bias = keep.tile([P, PACK], F32)
        nc.gpsimd.tensor_tensor(slope_th[:], sl_t[:], th_t[:], ALU.mult)
        nc.gpsimd.tensor_scalar(neg_bias[:], slope_th[:], -1.0, 0.0, ALU.mult, ALU.add)

        xs = keep.tile([P, S], U8, align_bytes=64)
        xw = keep.tile([P, S], U32, align_bytes=64)
        ds_got = keep.tile([P, 2 * H], U8, align_bytes=64)
        dw_got = keep.tile([P, 2 * H], U32, align_bytes=64)
        nc.vector.tensor_copy(xs[:], xs_win[:].indirect(offs_t[:]))
        nc.vector.tensor_copy(ds_got[:, 0:H], ds_win[:].indirect(ka_t[:]))
        nc.vector.tensor_copy(xw[:], xw_win[:].indirect(offs_t[:]))
        nc.vector.tensor_copy(ds_got[:, H : 2 * H], ds_win[:].indirect(kb_t[:]))

        y_ps = {}
        for t in PLANE_ORDER:
            y_ps[t] = psum.tile([P, S], F32, name=f"y_ps{t}", tag=f"bank{t}")
            nc.tensor.matmul_mx(
                out=y_ps[t][:],
                lhsT=w1w[:, 2 * P * t : 2 * P * (t + 1)].bitcast(FP4X4),
                lhsT_scale=w1s[:, P * t : P * (t + 1)],
                rhs=xw[:].bitcast(FP8X4),
                rhs_scale=xs[:],
                start=True,
                stop=True,
            )

        ds_dealt = keep.tile([P, 2 * H], U8, align_bytes=64)
        nc.vector.tensor_copy(dw_got[:, 0:H], dw_win[:].indirect(ka_t[:]))
        nc.vector.tensor_copy(
            ds_dealt[:].rearrange("p (a t m) -> p a t m", a=2, t=PACK),
            ds_got[:].rearrange("p (a m t) -> p a t m", a=2, t=PACK),
        )
        nc.vector.tensor_copy(dw_got[:, H : 2 * H], dw_win[:].indirect(kb_t[:]))
        for i in range(4):
            nc.sync.dma_start(ds_mm[i:P:32, :].bitcast(I32), ds_dealt[8 * i : P : 32, :].bitcast(I32))

        dw = keep.tile([P, 2 * H], U32, align_bytes=64)
        nc.vector.tensor_copy(
            dw[:].rearrange("p (a t m) -> p a m t", a=2, t=PACK),
            dw_got[:].rearrange("p (a m t) -> p a m t", a=2, t=PACK),
        )

        wide = {}
        y, pair, sums, ra, dt = {}, {}, {}, {}, {}
        a, b, c, d = PLANE_ORDER

        def leave_bank(t):
            y[t] = keep.tile([P, S], F32, name=f"y{t}", tag=f"y{PLANE_ORDER.index(t) % 2}", align_bytes=64)
            nc.scalar.copy(y[t][:], y_ps[t][:])

        def fetch_a(t):
            pair[t] = keep.tile([P, 2 * W], F32, name=f"pair{t}")
            nc.scalar.activation(pair[t][:, 0:W], y[t][:].indirect(n1_t[:]), ACT.Copy, scale=-0.5)

        def fetch_b(t):
            nc.scalar.activation(pair[t][:, W : 2 * W], y[t][:].indirect(n2_t[:]), ACT.Copy)

        def square(t):
            wide[t] = keep.tile([P, 2 * S], F32, name=f"wide{t}")
            nc.scalar.activation(wide[t][:, S : 2 * S], pair[t][:], ACT.Square)
            sums[t] = keep.tile([P, W], F32, name=f"sums{t}", tag=f"sums{t}", align_bytes=64)
            nc.vector.scalar_tensor_tensor(
                sums[t][:], wide[t][:, S : S + W], 4.0, wide[t][:, S + W : 2 * S], ALU.mult, ALU.add
            )

        def root(t):
            ra[t] = keep.tile([P, W], F32, name=f"ra{t}")
            nc.scalar.activation(ra[t][:], sums[t][:], ACT.Sqrt, bias=quarter[:])

        def put_rb(t):
            dt[t] = keep.tile([P, S], F32, name=f"dt{t}", tag="dw_win" if t == a else f"dt{t}", align_bytes=64)
            nc.vector.tensor_tensor(dt[t][:].indirect(n2_t[:]), pair[t][:, W : 2 * W], pair[t][:, 0:W], ALU.add)

        def put_ra(t):
            nc.vector.tensor_copy(dt[t][:].indirect(n1_t[:]), ra[t][:])

        def weigh(t, cols):
            nc.scalar.activation(zb[:, cols, t], dt[t][:, cols], ACT.Copy, scale=gs_t[:, t : t + 1])

        def weigh_on_vector(t, cols):
            nc.vector.tensor_scalar(zb[:, cols, t], dt[t][:, cols], gs_t[:, t : t + 1], None, ALU.mult)

        leave_bank(a)
        leave_bank(b)
        fetch_a(a)
        fetch_b(a)
        put_rb(a)
        fetch_a(b)
        square(a)
        fetch_b(b)
        put_rb(b)
        leave_bank(c)
        square(b)
        fetch_a(c)
        fetch_b(c)
        put_rb(c)
        leave_bank(d)
        square(c)
        root(a)
        put_ra(a)
        fetch_a(d)
        fetch_b(d)
        put_rb(d)
        root(b)
        put_ra(b)
        square(d)
        root(c)
        put_ra(c)
        root(d)
        halves = [slice(0, HALF), slice(HALF, S)]
        zb = keep.tile([P, S, PACK], BF16, tag=f"sums{c}", align_bytes=64)
        weigh(a, slice(0, S))
        weigh(b, slice(0, S))
        weigh(c, halves[1])
        weigh_on_vector(c, halves[0])
        put_ra(d)
        weigh(d, halves[1])
        weigh_on_vector(d, halves[0])
        warm_sigmoid = keep.tile([P, 1], F32)
        nc.scalar.activation(warm_sigmoid[:], dt[d][:, 0:1], ACT.Sigmoid, bias=quarter[:])

        zw = keep.tile([P, S], U32, align_bytes=64)
        zs = keep.tile([P, S], U8, align_bytes=64)
        for cols in halves:
            nc.vector.quantize_mx(
                out=zw[:, cols].bitcast(FP8X4),
                scales=zs[:, cols],
                in_=zb[:, cols, :].rearrange("p j t -> p (j t)"),
            )

        out_rows = out.rearrange("(p t) j -> p t j", t=PACK)
        h_ps, h, sg, res = {}, {}, {}, {}

        def product(t, cols, bank):
            for table in range(2):
                scols = slice(H * table + P * t, H * table + P * (t + 1))
                nc.tensor.matmul_mx(
                    out=bank,
                    lhsT=dw[:, scols].bitcast(FP8X4),
                    lhsT_scale=ds_mm[:, scols],
                    rhs=zw[:, cols].bitcast(FP8X4),
                    rhs_scale=zs[:, cols],
                    start=(table == 0),
                    stop=(table == 1),
                )

        for t in range(PACK):
            h_ps[t] = []
            for i, cols in enumerate(halves if t == 0 else [slice(0, S)]):
                bank = psum.tile([P, cols.stop - cols.start], F32, name=f"h_ps{t}_{i}", tag=f"bank{(4 + t + 4 * i) % 8}")
                product(t, cols, bank[:])
                h_ps[t].append((cols, bank))

        def evacuate(t):
            h[t] = wide[t] if t < PACK - 1 else keep.tile([P, S], F32, name=f"h{t}")
            for cols, bank in h_ps[t]:
                nc.vector.tensor_scalar(h[t][:, cols], bank[:], 0.0625, None, ALU.mult)

        def pieces(t):
            if t < PACK - 1:
                return [slice(0, S)]
            return [slice(0, HALF), slice(HALF, HALF + P), slice(HALF + P, S)]

        def gate(t):
            sg[t] = keep.tile([P, S], F32, name=f"sg{t}")
            for cols in pieces(t):
                nc.scalar.activation(
                    sg[t][:, cols],
                    h[t][:].indirect(n3_t[:, cols.start // 16 : cols.stop // 16]),
                    ACT.Sigmoid,
                    scale=sl_t[:, t : t + 1],
                    bias=neg_bias[:, t : t + 1],
                )

        def finish(t):
            res[t] = keep.tile([P, S], F32, name=f"res{t}")
            for cols in pieces(t):
                nc.vector.tensor_tensor(res[t][:, cols], h[t][:, cols], sg[t][:, cols], ALU.mult)
                nc.sync.dma_start(out_rows[:, t, cols], res[t][:, cols])

        evacuate(0)
        for t in range(PACK):
            gate(t)
            if t + 1 < PACK:
                evacuate(t + 1)
            finish(t)
